import numpy as np
import ml_dtypes


def mxq(x, axis, fmt="e4m3"):
    dtype, down = {"e4m3": (ml_dtypes.float8_e4m3fn, 7), "e5m2": (ml_dtypes.float8_e5m2, 14)}[fmt]
    v = np.moveaxis(np.asarray(x, np.float32).astype(ml_dtypes.bfloat16).astype(np.float64), axis, -1)
    blocks = v.reshape(v.shape[:-1] + (-1, 32))
    amax = np.abs(blocks).max(-1, keepdims=True)
    byte = np.maximum(np.where(amax > 0, np.frexp(amax)[1] - 1 + 127, 0) - down, 1)
    scale = np.exp2(byte - 127.0)
    codes = (blocks / scale).astype(np.float32).astype(dtype).astype(np.float64)
    return np.moveaxis((codes * scale).reshape(v.shape), -1, axis)


WIDE = False


def mx_kscale(k):
    if not WIDE:
        return np.ones(k)
    levels = np.array([30, -30])
    if k % 512:
        return np.exp2(np.random.permutation(np.resize(levels, k // 32))).repeat(32)
    a = np.empty((k // 512, 16))
    for p in range(k // 512):
        a[p, :8] = np.random.permutation(np.resize(levels, 8))
        for g in range(8):
            far = levels[np.abs(levels - a[p, g]) >= 10]
            a[p, g + 8] = far[np.random.randint(len(far))]
    return np.exp2(a.ravel()).repeat(32)


def f64(x):
    return np.asarray(x).astype(np.float64)


def striped(idx):
    return np.tile(np.asarray(idx).reshape(-1, 16).T, (8, 1)).astype(np.uint16)


def unstriped(offs):
    return offs[:16].T.reshape(-1).astype(np.int64)


E2M1 = np.array([0.0, 0.5, 1.0, 1.5, 2.0, 3.0, 4.0, 6.0, -0.0, -0.5, -1.0, -1.5, -2.0, -3.0, -4.0, -6.0])


def pack_weight(w, fmt):
    k, n = w.shape
    w = f64(np.asarray(w, np.float32).astype(ml_dtypes.bfloat16)).reshape(k // 32, 32, n)
    amax = np.abs(w).max(1)
    if fmt in ("e4m3", "e5m2"):
        byte = np.frexp(amax)[1] - 1 + 127 - (7 if fmt == "e4m3" else 14)
    else:
        mant, ex = np.frexp(amax / 6.0)
        byte = np.where(mant > 0.5, ex, ex - 1) + 127
    byte = np.clip(np.where(amax > 0, byte, 1), 1, 254)
    scaled = (w * np.exp2(127.0 - byte)[:, None, :]).reshape(k, n).astype(np.float32)
    by_word = np.ascontiguousarray(scaled.reshape(k // 512, 128, 4, n).transpose(0, 1, 3, 2))
    if fmt in ("e4m3", "e5m2"):
        words = by_word.astype(ml_dtypes.float8_e4m3fn if fmt == "e4m3" else ml_dtypes.float8_e5m2).view(np.uint8)
    else:
        c = by_word.astype(ml_dtypes.float4_e2m1fn).view(np.uint8) & 0xF
        words = (c[..., 0::2] | (c[..., 1::2] << 4)).reshape(k // 512, 128, 2 * n)
    return np.ascontiguousarray(words), np.ascontiguousarray(byte.astype(np.uint8).reshape(k // 512, 16, n))


def unpack_weight(words, scales, fmt):
    g, _, n = scales.shape
    words = np.ascontiguousarray(words).reshape(g, 128, n, -1)
    if fmt in ("e4m3", "e5m2"):
        vals = words.view(ml_dtypes.float8_e4m3fn if fmt == "e4m3" else ml_dtypes.float8_e5m2).astype(np.float64)
    else:
        nib = np.empty((g, 128, n, 4), np.uint8)
        nib[..., 0::2] = words & 0xF
        nib[..., 1::2] = words >> 4
        vals = E2M1[nib]
    vals = vals * np.repeat(np.exp2(scales.astype(np.float64) - 127.0), 8, axis=1)[..., None]
    return vals.transpose(0, 1, 3, 2).reshape(g * 512, n)


def bf(x):
    return np.asarray(x, np.float32).astype(ml_dtypes.bfloat16)


def planes(Y):
    r, m = Y.shape
    b = f64(bf(Y)).reshape(r // 32, 32, m)
    amax = np.abs(b).max(1)
    byte = np.clip(np.where(amax > 0, np.frexp(amax)[1] - 1 + 127 - 7, 1), 1, 254)
    codes = (b * np.exp2(127.0 - byte)[:, None, :]).reshape(r, m).astype(np.float32).astype(ml_dtypes.float8_e4m3fn).view(np.uint8)
    words = codes.reshape(r // 512, 128, 4, m).transpose(0, 1, 3, 2)
    return np.ascontiguousarray(words), np.ascontiguousarray(byte.astype(np.uint8).reshape(r // 512, 16, m))


K, T, J, I, L, S, R, G, N = 1024, 1024, 256, 128, 128, 512, 512, 128, 512


def setup_inputs():
    n = np.random.standard_normal
    idx = np.random.permutation(T)[:I]
    idx2 = np.random.permutation(S)[:L]
    fk = mx_kscale(K)
    fr = mx_kscale(R)
    wp = pack_weight(n((K, R)) * 1 / np.sqrt(K) * fk[:, None] * fr, "e5m2")
    return {
        "xa": (n((K, T)) / fk[:, None]).astype(np.float32),
        "xb": (n((K, S)) * 0.6 / fk[:, None]).astype(np.float32),
        "w_words": wp[0],
        "w_scales": wp[1],
        "wb": (n((R, N)) * 1 / np.sqrt(R) / fr[:, None]).astype(np.float32),
        "hi": (np.random.uniform(0.4, 1.2, (N, 1))).astype(np.float32),
        "rw": (np.random.uniform(0.5, 2.0, (1, G))).astype(np.float32),
        "offs": striped(idx),
        "offs2": striped(idx2),
    }


def reference(xa, xb, w_words, w_scales, wb, hi, rw, offs, offs2):
    idx = unstriped(offs)
    idx2 = unstriped(offs2)
    wu = unpack_weight(w_words, w_scales, "e5m2")
    u = np.concatenate([f64(xa)[:, idx], f64(xb)[:, idx2]], axis=1)
    uq = mxq(u, 0, "e4m3")
    a = wu.T @ uq
    hid = a.reshape(R, G, J // G).max(axis=2)
    wbq = mxq(f64(wb), 0, "e4m3")
    hidq = mxq(hid, 0, "e5m2")
    p = wbq.T @ hidq
    y = np.minimum(p - f64(hi), 0.0) * f64(rw)
    words, scales = planes(y)
    return y, words, scales

@@ -1,0 +1,199 @@
+from contextlib import ExitStack
+
+import concourse.mybir as mybir
+from concourse.masks import make_identity
+
+K, T, S, R, G, N = 1024, 1024, 512, 512, 128, 512
+SLOTS = 128
+FLOPS = 2 * K * R * 2 * SLOTS + 2 * R * N * G
+
+F32 = mybir.dt.float32
+BF16 = mybir.dt.bfloat16
+I32 = mybir.dt.int32
+U16 = mybir.dt.uint16
+U8 = mybir.dt.uint8
+E4M3 = mybir.dt.float8_e4m3fn_x4
+E5M2 = mybir.dt.float8_e5m2_x4
+ALU = mybir.AluOpType
+ACT = mybir.ActivationFunctionType
+
+P = 128
+PACK = 4
+K_PASS = P * PACK
+PASSES = K // K_PASS
+HALF_M = P // 2
+HALF_G = G // 2
+
+
+def tile_list_joined_pooled_capped_pl_kernel(tc, xa, xb, w_words, w_scales, wb, hi, rw, offs, offs2, out_0, out_1, out_2):
+    nc = tc.nc
+    with ExitStack() as ctx:
+        sb = ctx.enter_context(tc.tile_pool(name="sb", bufs=1))
+        ps = ctx.enter_context(tc.psum_pool(name="ps", bufs=1))
+
+        def load_planes(x, name, a, first, count):
+            rows = x[a * K_PASS : (a + 1) * K_PASS, :].rearrange("(p i) c -> p i c", i=PACK)
+            tile = sb.tile([P, count, x.shape[1]], F32, name=name)
+            nc.sync.dma_start(out=tile[:], in_=rows[:, first : first + count, :])
+            return [tile[:, i, :] for i in range(count)]
+
+        def load_wb(name, first, count):
+            tile = sb.tile([P, PACK, count], F32, name=name)
+            nc.sync.dma_start(out=tile[:], in_=wb.rearrange("(p j) n -> p j n", j=PACK)[:, :, first : first + count])
+            return tile
+
+        list_b = sb.tile([P, SLOTS // 16], U16, name="list_b")
+        nc.sync.dma_start(list_b[:], offs2)
+        xb_planes = [load_planes(xb, "xb0", 0, 0, PACK)]
+        list_a = sb.tile([P, SLOTS // 16], U16, name="list_a")
+        nc.sync.dma_start(list_a[:], offs)
+        xb_planes.append(load_planes(xb, "xb1", 1, 0, PACK))
+
+        w_scales_raw = sb.tile([P, PASSES, R], U8, name="w_scales_raw")
+        nc.vector.memset(w_scales_raw[:].bitcast(I32), 0)
+        for q in range(4):
+            nc.scalar.dma_start(
+                out=w_scales_raw[32 * q : 32 * q + 4].bitcast(I32),
+                in_=w_scales[:, 4 * q : 4 * q + 4, :].rearrange("a r c -> r a c").bitcast(I32),
+            )
+        hi_sb = sb.tile([P, PACK], F32, name="hi_sb")
+        nc.scalar.dma_start(out=hi_sb[:], in_=hi.rearrange("(p t) o -> p (t o)", t=PACK))
+        rw_col = sb.tile([P, 1], F32, name="rw_col")
+        with nc.allow_non_contiguous_dma(reason="one weight to a partition"):
+            nc.scalar.dma_start(out=rw_col[:], in_=rw.rearrange("o g -> g o"))
+
+        w_words_raw = sb.tile([P, PASSES, R], I32, name="w_words_raw")
+        nc.sync.dma_start(out=w_words_raw[:], in_=w_words.rearrange("a p c t -> p a (c t)").bitcast(I32))
+        wb_raw = [(load_wb("wb_raw0", 0, 256), 0, 0)]
+        xa_planes = [
+            load_planes(xa, "xa00", 0, 0, 2) + load_planes(xa, "xa01", 0, 2, 2),
+            load_planes(xa, "xa10", 1, 0, 2) + load_planes(xa, "xa11", 1, 2, 1) + load_planes(xa, "xa12", 1, 3, 1),
+        ]
+        wb_raw.append((load_wb("wb_raw1", 256, 128), 1, 0))
+        wb_raw.append((load_wb("wb_raw2", 384, 128), 1, 32))
+
+        neg_hi = sb.tile([P, PACK], F32, name="neg_hi")
+        nc.scalar.mul(neg_hi[:], hi_sb[:], -1.0)
+        ident = sb.tile([P, P], F32, name="ident")
+        make_identity(nc, ident[:])
+        rw_rows = ps.tile([P, G], F32, name="rw_rows")
+        nc.tensor.transpose(rw_rows[:], rw_col[:, 0:1].to_broadcast([P, P]), ident[:])
+
+        def gather_quantise(planes, offsets, name):
+            picked = sb.tile([P, SLOTS, PACK], BF16, name=name + "_bf", align_bytes=64)
+            for i in range(PACK):
+                nc.vector.tensor_copy(out=picked[:, :, i], in_=planes[i].indirect(offsets[:]))
+            codes = sb.tile([P, SLOTS], I32, name=name + "_codes", align_bytes=64)
+            scales = sb.tile([P, SLOTS], U8, name=name + "_scales", align_bytes=64)
+            nc.vector.quantize_mx(out=codes[:].bitcast(E4M3), scales=scales[:], in_=picked[:].rearrange("p j i -> p (j i)"))
+            return codes, scales
+
+        ub = [gather_quantise(xb_planes[a], list_b, "ub%d" % a) for a in range(PASSES)]
+
+        w_codes = sb.tile([P, PASSES, PACK, P], I32, name="w_codes", align_bytes=64)
+        w_sc = sb.tile([P, PASSES, PACK, P], U8, name="w_sc", align_bytes=64)
+        nc.vector.tensor_copy(out=w_codes[:], in_=w_words_raw[:].rearrange("p a (m t) -> p a t m", t=PACK))
+        nc.vector.tensor_copy(out=w_sc[:], in_=w_scales_raw[:].rearrange("p a (m t) -> p a t m", t=PACK))
+
+        def first_product(out, a, t, u, start, stop):
+            nc.tensor.matmul_mx(
+                out=out,
+                lhsT=w_codes[:, a, t, :].bitcast(E5M2),
+                lhsT_scale=w_sc[:, a, t, :],
+                rhs=u[0][:].bitcast(E4M3),
+                rhs_scale=u[1][:],
+                start=start,
+                stop=stop,
+            )
+
+        hid_codes = sb.tile([P, G], I32, name="hid_codes", align_bytes=64)
+        hid_scales = sb.tile([P, G], U8, name="hid_scales", align_bytes=64)
+
+        def quantise_hid(hid, first):
+            nc.vector.quantize_mx(
+                out=hid_codes[:, first : first + HALF_G].bitcast(E5M2),
+                scales=hid_scales[:, first : first + HALF_G],
+                in_=hid[:].rearrange("p g t -> p (g t)"),
+            )
+
+        acc_b = ps.tile([P, PACK, SLOTS], F32, name="acc_b")
+        for t in range(PACK):
+            for a in range(PASSES):
+                first_product(acc_b[:, t, :], a, t, ub[a], a == 0, a == PASSES - 1)
+        hid_b = sb.tile([P, HALF_G, PACK], BF16, name="hid_b", align_bytes=64)
+        nc.vector.tensor_reduce(
+            out=hid_b[:], in_=acc_b[:].rearrange("p t (g e) -> p g t e", e=2), axis=mybir.AxisListType.X, op=ALU.max
+        )
+        quantise_hid(hid_b, HALF_G)
+
+        wb_bf = [sb.tile([P, PACK, HALF_M, PACK], BF16, name="wb_bf%d" % h, align_bytes=64) for h in range(2)]
+        wb_codes = sb.tile([P, PACK, P], I32, name="wb_codes", align_bytes=64)
+        wb_scales = sb.tile([P, PACK, P], U8, name="wb_scales", align_bytes=64)
+
+        def round_wb(raw, h, m0):
+            count = raw.shape[2] // PACK
+            nc.scalar.copy(
+                out=wb_bf[h][:, :, m0 : m0 + count, :].rearrange("p t m j -> p m t j"),
+                in_=raw[:].rearrange("p j (m t) -> p m t j", t=PACK),
+            )
+
+        def quantise_wb(h, t):
+            cols = slice(h * HALF_M, (h + 1) * HALF_M)
+            nc.vector.quantize_mx(
+                out=wb_codes[:, t, cols].bitcast(E4M3),
+                scales=wb_scales[:, t, cols],
+                in_=wb_bf[h][:, t, :, :].rearrange("p m j -> p (m j)"),
+            )
+
+        round_wb(*wb_raw[0])
+        for t in range(PACK):
+            quantise_wb(0, t)
+
+        acc_a = [ps.tile([P, 2, SLOTS], F32, name="acc_a%d" % v) for v in range(2)]
+        hid_a = sb.tile([P, HALF_G, PACK], BF16, name="hid_a", align_bytes=64)
+        for a in range(PASSES):
+            ua = gather_quantise(xa_planes[a], list_a, "ua%d" % a)
+            for t in range(PACK):
+                first_product(acc_a[t // 2][:, t % 2, :], a, t, ua, a == 0 and t % 2 == 0, a == PASSES - 1 and t % 2 == 1)
+        for v in range(2):
+            nc.vector.tensor_reduce(
+                out=hid_a[:, :, 2 * v : 2 * v + 2],
+                in_=acc_a[v][:].rearrange("p t (g e) -> p g t e", e=2),
+                axis=mybir.AxisListType.X,
+                op=ALU.max,
+            )
+        quantise_hid(hid_a, 0)
+
+        round_wb(*wb_raw[1])
+        round_wb(*wb_raw[2])
+        for t in range(PACK):
+            quantise_wb(1, t)
+
+        diff = sb.tile([P, PACK, G], F32, name="diff")
+        y = sb.tile([P, PACK, G], F32, name="y")
+        for t in range(PACK):
+            acc_p = ps.tile([P, G], F32, name="acc_p%d" % t)
+            nc.tensor.matmul_mx(
+                out=acc_p[:],
+                lhsT=wb_codes[:, t, :].bitcast(E4M3),
+                lhsT_scale=wb_scales[:, t, :],
+                rhs=hid_codes[:].bitcast(E5M2),
+                rhs_scale=hid_scales[:],
+                start=True,
+                stop=True,
+            )
+            nc.scalar.activation(out=diff[:, t, :], in_=acc_p[:], func=ACT.Identity, bias=neg_hi[:, t : t + 1], scale=1.0)
+            nc.vector.scalar_tensor_tensor(
+                out=y[:, t, :], in0=diff[:, t, :], scalar=0.0, in1=rw_rows[:], op0=ALU.min, op1=ALU.mult
+            )
+        nc.sync.dma_start(out=out_0.rearrange("(p t) g -> p t g", t=PACK), in_=y[:])
+
+        y_bf = sb.tile([P, G, PACK], BF16, name="y_bf", align_bytes=64)
+        nc.vector.tensor_copy(out=y_bf[:], in_=y[:].rearrange("p t g -> p g t"))
+        y_codes = sb.tile([P, G], I32, name="y_codes", align_bytes=64)
+        y_scales = sb.tile([P, G], U8, name="y_scales", align_bytes=64)
+        nc.vector.quantize_mx(out=y_codes[:].bitcast(E4M3), scales=y_scales[:], in_=y_bf[:].rearrange("p g t -> p (g t)"))
+        nc.sync.dma_start(out=out_1[0].rearrange("p g t -> p (g t)").bitcast(I32), in_=y_codes[:])
+        for q in range(4):
+            queue = nc.scalar if q < 2 else nc.sync
+            queue.dma_start(out=out_2[0, 4 * q : 4 * q + 4, :].bitcast(I32), in_=y_scales[32 * q : 32 * q + 4, :].bitcast(I32))

@@ -44,16 +44,18 @@ def tile_list_joined_pooled_capped_pl_kernel(tc, xa, xb, w_words, w_scales, wb, 
 
         list_b = sb.tile([P, SLOTS // 16], U16, name="list_b")
         nc.sync.dma_start(list_b[:], offs2)
-        xb_planes = [load_planes(xb, "xb0", 0, 0, PACK)]
+        xb_sb = sb.tile([P, PASSES, PACK * S], F32, name="xb_sb")
+        nc.sync.dma_start(out=xb_sb[:], in_=xb.rearrange("(a p i) c -> p a (i c)", a=PASSES, i=PACK))
+        xb_planes = [[xb_sb[:, a, i * S : (i + 1) * S] for i in range(PACK)] for a in range(PASSES)]
+        w_words_raw = sb.tile([P, PASSES, R], I32, name="w_words_raw")
+        nc.sync.dma_start(out=w_words_raw[:], in_=w_words.rearrange("a p c t -> p a (c t)").bitcast(I32))
+        xa_planes = [load_planes(xa, "xa0", 0, 0, PACK)]
         list_a = sb.tile([P, SLOTS // 16], U16, name="list_a")
         nc.sync.dma_start(list_a[:], offs)
-        xb_planes.append(load_planes(xb, "xb1", 1, 0, PACK))
-
-        w_scales_raw = sb.tile([P, PASSES, R], U8, name="w_scales_raw")
-        nc.vector.memset(w_scales_raw[:].bitcast(I32), 0)
+        w_scale_rows = sb.tile([P, PASSES, R // 4], I32, name="w_scale_rows")
         for q in range(4):
             nc.scalar.dma_start(
-                out=w_scales_raw[32 * q : 32 * q + 4].bitcast(I32),
+                out=w_scale_rows[32 * q : 32 * q + 4],
                 in_=w_scales[:, 4 * q : 4 * q + 4, :].rearrange("a r c -> r a c").bitcast(I32),
             )
         hi_sb = sb.tile([P, PACK], F32, name="hi_sb")
@@ -61,16 +63,13 @@ def tile_list_joined_pooled_capped_pl_kernel(tc, xa, xb, w_words, w_scales, wb, 
         rw_col = sb.tile([P, 1], F32, name="rw_col")
         with nc.allow_non_contiguous_dma(reason="one weight to a partition"):
             nc.scalar.dma_start(out=rw_col[:], in_=rw.rearrange("o g -> g o"))
-
-        w_words_raw = sb.tile([P, PASSES, R], I32, name="w_words_raw")
-        nc.sync.dma_start(out=w_words_raw[:], in_=w_words.rearrange("a p c t -> p a (c t)").bitcast(I32))
-        wb_raw = [(load_wb("wb_raw0", 0, 256), 0, 0)]
-        xa_planes = [
-            load_planes(xa, "xa00", 0, 0, 2) + load_planes(xa, "xa01", 0, 2, 2),
-            load_planes(xa, "xa10", 1, 0, 2) + load_planes(xa, "xa11", 1, 2, 1) + load_planes(xa, "xa12", 1, 3, 1),
-        ]
-        wb_raw.append((load_wb("wb_raw1", 256, 128), 1, 0))
-        wb_raw.append((load_wb("wb_raw2", 384, 128), 1, 32))
+        wb_raw = [(load_wb("wb_raw0", 0, 192), 0, 0)]
+        xa_planes.append(
+            load_planes(xa, "xa10", 1, 0, 2) + load_planes(xa, "xa11", 1, 2, 1) + load_planes(xa, "xa12", 1, 3, 1)
+        )
+        wb_raw.append((load_wb("wb_raw1", 192, 64), 0, 48))
+        wb_raw.append((load_wb("wb_raw2", 256, 128), 1, 0))
+        wb_raw.append((load_wb("wb_raw3", 384, 128), 1, 32))
 
         neg_hi = sb.tile([P, PACK], F32, name="neg_hi")
         nc.scalar.mul(neg_hi[:], hi_sb[:], -1.0)
@@ -79,21 +78,36 @@ def tile_list_joined_pooled_capped_pl_kernel(tc, xa, xb, w_words, w_scales, wb, 
         rw_rows = ps.tile([P, G], F32, name="rw_rows")
         nc.tensor.transpose(rw_rows[:], rw_col[:, 0:1].to_broadcast([P, P]), ident[:])
 
-        def gather_quantise(planes, offsets, name):
+        def gather_on_scalar(planes, offsets, name):
+            rows = sb.tile([P, PACK, SLOTS], F32, name=name + "_rows")
+            for i in range(PACK):
+                nc.scalar.activation(out=rows[:, i, :], in_=planes[i].indirect(offsets[:]), func=ACT.Copy)
+            picked = sb.tile([P, SLOTS, PACK], BF16, name=name + "_bf", align_bytes=64)
+            nc.vector.tensor_copy(out=picked[:], in_=rows[:].rearrange("p i j -> p j i"))
+            return picked
+
+        def gather_on_vector(planes, offsets, name):
             picked = sb.tile([P, SLOTS, PACK], BF16, name=name + "_bf", align_bytes=64)
             for i in range(PACK):
                 nc.vector.tensor_copy(out=picked[:, :, i], in_=planes[i].indirect(offsets[:]))
+            return picked
+
+        def quantise_u(picked, name):
             codes = sb.tile([P, SLOTS], I32, name=name + "_codes", align_bytes=64)
             scales = sb.tile([P, SLOTS], U8, name=name + "_scales", align_bytes=64)
             nc.vector.quantize_mx(out=codes[:].bitcast(E4M3), scales=scales[:], in_=picked[:].rearrange("p j i -> p (j i)"))
             return codes, scales
 
-        ub = [gather_quantise(xb_planes[a], list_b, "ub%d" % a) for a in range(PASSES)]
-
+        w_scales_raw = sb.tile([P, PASSES, R], U8, name="w_scales_raw")
+        nc.vector.memset(w_scales_raw[:].bitcast(I32), 0)
+        for q in range(4):
+            nc.vector.tensor_copy(out=w_scales_raw[32 * q : 32 * q + 4].bitcast(I32), in_=w_scale_rows[32 * q : 32 * q + 4])
         w_codes = sb.tile([P, PASSES, PACK, P], I32, name="w_codes", align_bytes=64)
         w_sc = sb.tile([P, PASSES, PACK, P], U8, name="w_sc", align_bytes=64)
         nc.vector.tensor_copy(out=w_codes[:], in_=w_words_raw[:].rearrange("p a (m t) -> p a t m", t=PACK))
         nc.vector.tensor_copy(out=w_sc[:], in_=w_scales_raw[:].rearrange("p a (m t) -> p a t m", t=PACK))
+
+        ub = [quantise_u(gather_on_scalar(xb_planes[a], list_b, "ub%d" % a), "ub%d" % a) for a in range(PASSES)]
 
         def first_product(out, a, t, u, start, stop):
             nc.tensor.matmul_mx(
@@ -146,13 +160,16 @@ def tile_list_joined_pooled_capped_pl_kernel(tc, xa, xb, w_words, w_scales, wb, 
             )
 
         round_wb(*wb_raw[0])
-        for t in range(PACK):
-            quantise_wb(0, t)
 
         acc_a = [ps.tile([P, 2, SLOTS], F32, name="acc_a%d" % v) for v in range(2)]
         hid_a = sb.tile([P, HALF_G, PACK], BF16, name="hid_a", align_bytes=64)
         for a in range(PASSES):
-            ua = gather_quantise(xa_planes[a], list_a, "ua%d" % a)
+            gather = gather_on_vector if a == PASSES - 1 else gather_on_scalar
+            ua = quantise_u(gather(xa_planes[a], list_a, "ua%d" % a), "ua%d" % a)
+            if a == PASSES - 1:
+                round_wb(*wb_raw[1])
+                for t in range(PACK):
+                    quantise_wb(0, t)
             for t in range(PACK):
                 first_product(acc_a[t // 2][:, t % 2, :], a, t, ua, a == 0 and t % 2 == 0, a == PASSES - 1 and t % 2 == 1)
         for v in range(2):
@@ -164,8 +181,8 @@ def tile_list_joined_pooled_capped_pl_kernel(tc, xa, xb, w_words, w_scales, wb, 
             )
         quantise_hid(hid_a, 0)
 
-        round_wb(*wb_raw[1])
         round_wb(*wb_raw[2])
+        round_wb(*wb_raw[3])
         for t in range(PACK):
             quantise_wb(1, t)
 
@@ -189,7 +206,8 @@ def tile_list_joined_pooled_capped_pl_kernel(tc, xa, xb, w_words, w_scales, wb, 
         nc.sync.dma_start(out=out_0.rearrange("(p t) g -> p t g", t=PACK), in_=y[:])
 
         y_bf = sb.tile([P, G, PACK], BF16, name="y_bf", align_bytes=64)
-        nc.vector.tensor_copy(out=y_bf[:], in_=y[:].rearrange("p t g -> p g t"))
+        for v in range(2):
+            nc.vector.tensor_copy(out=y_bf[:, :, 2 * v : 2 * v + 2], in_=y[:, 2 * v : 2 * v + 2, :].rearrange("p t g -> p g t"))
         y_codes = sb.tile([P, G], I32, name="y_codes", align_bytes=64)
         y_scales = sb.tile([P, G], U8, name="y_scales", align_bytes=64)
         nc.vector.quantize_mx(out=y_codes[:].bitcast(E4M3), scales=y_scales[:], in_=y_bf[:].rearrange("p g t -> p (g t)"))

from contextlib import ExitStack

import concourse.mybir as mybir
from concourse.masks import make_identity

K, T, S, R, G, N = 1024, 1024, 512, 512, 128, 512
SLOTS = 128
FLOPS = 2 * K * R * 2 * SLOTS + 2 * R * N * G

F32 = mybir.dt.float32
BF16 = mybir.dt.bfloat16
I32 = mybir.dt.int32
U16 = mybir.dt.uint16
U8 = mybir.dt.uint8
E4M3 = mybir.dt.float8_e4m3fn_x4
E5M2 = mybir.dt.float8_e5m2_x4
ALU = mybir.AluOpType
ACT = mybir.ActivationFunctionType

P = 128
PACK = 4
K_PASS = P * PACK
PASSES = K // K_PASS
HALF_M = P // 2
HALF_G = G // 2


def tile_list_joined_pooled_capped_pl_kernel(tc, xa, xb, w_words, w_scales, wb, hi, rw, offs, offs2, out_0, out_1, out_2):
    nc = tc.nc
    with ExitStack() as ctx:
        sb = ctx.enter_context(tc.tile_pool(name="sb", bufs=1))
        ps = ctx.enter_context(tc.psum_pool(name="ps", bufs=1))

        def load_planes(x, name, a, first, count):
            rows = x[a * K_PASS : (a + 1) * K_PASS, :].rearrange("(p i) c -> p i c", i=PACK)
            tile = sb.tile([P, count, x.shape[1]], F32, name=name)
            nc.sync.dma_start(out=tile[:], in_=rows[:, first : first + count, :])
            return [tile[:, i, :] for i in range(count)]

        def load_wb(name, first, count):
            tile = sb.tile([P, PACK, count], F32, name=name)
            nc.sync.dma_start(out=tile[:], in_=wb.rearrange("(p j) n -> p j n", j=PACK)[:, :, first : first + count])
            return tile

        list_b = sb.tile([P, SLOTS // 16], U16, name="list_b")
        nc.sync.dma_start(list_b[:], offs2)
        xb_sb = sb.tile([P, PASSES, PACK * S], F32, name="xb_sb")
        nc.sync.dma_start(out=xb_sb[:], in_=xb.rearrange("(a p i) c -> p a (i c)", a=PASSES, i=PACK))
        xb_planes = [[xb_sb[:, a, i * S : (i + 1) * S] for i in range(PACK)] for a in range(PASSES)]
        w_words_raw = sb.tile([P, PASSES, R], I32, name="w_words_raw")
        nc.sync.dma_start(out=w_words_raw[:], in_=w_words.rearrange("a p c t -> p a (c t)").bitcast(I32))
        xa_planes = [load_planes(xa, "xa0", 0, 0, PACK)]
        list_a = sb.tile([P, SLOTS // 16], U16, name="list_a")
        nc.sync.dma_start(list_a[:], offs)
        w_scale_rows = sb.tile([P, PASSES, R // 4], I32, name="w_scale_rows")
        for q in range(4):
            nc.scalar.dma_start(
                out=w_scale_rows[32 * q : 32 * q + 4],
                in_=w_scales[:, 4 * q : 4 * q + 4, :].rearrange("a r c -> r a c").bitcast(I32),
            )
        hi_sb = sb.tile([P, PACK], F32, name="hi_sb")
        nc.scalar.dma_start(out=hi_sb[:], in_=hi.rearrange("(p t) o -> p (t o)", t=PACK))
        rw_col = sb.tile([P, 1], F32, name="rw_col")
        with nc.allow_non_contiguous_dma(reason="one weight to a partition"):
            nc.scalar.dma_start(out=rw_col[:], in_=rw.rearrange("o g -> g o"))
        wb_raw = [(load_wb("wb_raw0", 0, 192), 0, 0)]
        xa_planes.append(
            load_planes(xa, "xa10", 1, 0, 2) + load_planes(xa, "xa11", 1, 2, 1) + load_planes(xa, "xa12", 1, 3, 1)
        )
        wb_raw.append((load_wb("wb_raw1", 192, 64), 0, 48))
        wb_raw.append((load_wb("wb_raw2", 256, 128), 1, 0))
        wb_raw.append((load_wb("wb_raw3", 384, 128), 1, 32))

        neg_hi = sb.tile([P, PACK], F32, name="neg_hi")
        nc.scalar.mul(neg_hi[:], hi_sb[:], -1.0)
        ident = sb.tile([P, P], F32, name="ident")
        make_identity(nc, ident[:])
        rw_rows = ps.tile([P, G], F32, name="rw_rows")
        nc.tensor.transpose(rw_rows[:], rw_col[:, 0:1].to_broadcast([P, P]), ident[:])

        def gather_on_scalar(planes, offsets, name):
            rows = sb.tile([P, PACK, SLOTS], F32, name=name + "_rows")
            for i in range(PACK):
                nc.scalar.activation(out=rows[:, i, :], in_=planes[i].indirect(offsets[:]), func=ACT.Copy)
            picked = sb.tile([P, SLOTS, PACK], BF16, name=name + "_bf", align_bytes=64)
            nc.vector.tensor_copy(out=picked[:], in_=rows[:].rearrange("p i j -> p j i"))
            return picked

        def gather_on_vector(planes, offsets, name):
            picked = sb.tile([P, SLOTS, PACK], BF16, name=name + "_bf", align_bytes=64)
            for i in range(PACK):
                nc.vector.tensor_copy(out=picked[:, :, i], in_=planes[i].indirect(offsets[:]))
            return picked

        def quantise_u(picked, name):
            codes = sb.tile([P, SLOTS], I32, name=name + "_codes", align_bytes=64)
            scales = sb.tile([P, SLOTS], U8, name=name + "_scales", align_bytes=64)
            nc.vector.quantize_mx(out=codes[:].bitcast(E4M3), scales=scales[:], in_=picked[:].rearrange("p j i -> p (j i)"))
            return codes, scales

        w_scales_raw = sb.tile([P, PASSES, R], U8, name="w_scales_raw")
        nc.vector.memset(w_scales_raw[:].bitcast(I32), 0)
        for q in range(4):
            nc.vector.tensor_copy(out=w_scales_raw[32 * q : 32 * q + 4].bitcast(I32), in_=w_scale_rows[32 * q : 32 * q + 4])
        w_codes = sb.tile([P, PASSES, PACK, P], I32, name="w_codes", align_bytes=64)
        w_sc = sb.tile([P, PASSES, PACK, P], U8, name="w_sc", align_bytes=64)
        nc.vector.tensor_copy(out=w_codes[:], in_=w_words_raw[:].rearrange("p a (m t) -> p a t m", t=PACK))
        nc.vector.tensor_copy(out=w_sc[:], in_=w_scales_raw[:].rearrange("p a (m t) -> p a t m", t=PACK))

        ub = [quantise_u(gather_on_scalar(xb_planes[a], list_b, "ub%d" % a), "ub%d" % a) for a in range(PASSES)]

        def first_product(out, a, t, u, start, stop):
            nc.tensor.matmul_mx(
                out=out,
                lhsT=w_codes[:, a, t, :].bitcast(E5M2),
                lhsT_scale=w_sc[:, a, t, :],
                rhs=u[0][:].bitcast(E4M3),
                rhs_scale=u[1][:],
                start=start,
                stop=stop,
            )

        hid_codes = sb.tile([P, G], I32, name="hid_codes", align_bytes=64)
        hid_scales = sb.tile([P, G], U8, name="hid_scales", align_bytes=64)

        def quantise_hid(hid, first):
            nc.vector.quantize_mx(
                out=hid_codes[:, first : first + HALF_G].bitcast(E5M2),
                scales=hid_scales[:, first : first + HALF_G],
                in_=hid[:].rearrange("p g t -> p (g t)"),
            )

        acc_b = ps.tile([P, PACK, SLOTS], F32, name="acc_b")
        for t in range(PACK):
            for a in range(PASSES):
                first_product(acc_b[:, t, :], a, t, ub[a], a == 0, a == PASSES - 1)
        hid_b = sb.tile([P, HALF_G, PACK], BF16, name="hid_b", align_bytes=64)
        nc.vector.tensor_reduce(
            out=hid_b[:], in_=acc_b[:].rearrange("p t (g e) -> p g t e", e=2), axis=mybir.AxisListType.X, op=ALU.max
        )
        quantise_hid(hid_b, HALF_G)

        wb_bf = [sb.tile([P, PACK, HALF_M, PACK], BF16, name="wb_bf%d" % h, align_bytes=64) for h in range(2)]
        wb_codes = sb.tile([P, PACK, P], I32, name="wb_codes", align_bytes=64)
        wb_scales = sb.tile([P, PACK, P], U8, name="wb_scales", align_bytes=64)

        def round_wb(raw, h, m0):
            count = raw.shape[2] // PACK
            nc.scalar.copy(
                out=wb_bf[h][:, :, m0 : m0 + count, :].rearrange("p t m j -> p m t j"),
                in_=raw[:].rearrange("p j (m t) -> p m t j", t=PACK),
            )

        def quantise_wb(h, t):
            cols = slice(h * HALF_M, (h + 1) * HALF_M)
            nc.vector.quantize_mx(
                out=wb_codes[:, t, cols].bitcast(E4M3),
                scales=wb_scales[:, t, cols],
                in_=wb_bf[h][:, t, :, :].rearrange("p m j -> p (m j)"),
            )

        round_wb(*wb_raw[0])

        acc_a = [ps.tile([P, 2, SLOTS], F32, name="acc_a%d" % v) for v in range(2)]
        hid_a = sb.tile([P, HALF_G, PACK], BF16, name="hid_a", align_bytes=64)
        for a in range(PASSES):
            gather = gather_on_vector if a == PASSES - 1 else gather_on_scalar
            ua = quantise_u(gather(xa_planes[a], list_a, "ua%d" % a), "ua%d" % a)
            if a == PASSES - 1:
                round_wb(*wb_raw[1])
                for t in range(PACK):
                    quantise_wb(0, t)
            for t in range(PACK):
                first_product(acc_a[t // 2][:, t % 2, :], a, t, ua, a == 0 and t % 2 == 0, a == PASSES - 1 and t % 2 == 1)
        for v in range(2):
            nc.vector.tensor_reduce(
                out=hid_a[:, :, 2 * v : 2 * v + 2],
                in_=acc_a[v][:].rearrange("p t (g e) -> p g t e", e=2),
                axis=mybir.AxisListType.X,
                op=ALU.max,
            )
        quantise_hid(hid_a, 0)

        round_wb(*wb_raw[2])
        round_wb(*wb_raw[3])
        for t in range(PACK):
            quantise_wb(1, t)

        diff = sb.tile([P, PACK, G], F32, name="diff")
        y = sb.tile([P, PACK, G], F32, name="y")
        for t in range(PACK):
            acc_p = ps.tile([P, G], F32, name="acc_p%d" % t)
            nc.tensor.matmul_mx(
                out=acc_p[:],
                lhsT=wb_codes[:, t, :].bitcast(E4M3),
                lhsT_scale=wb_scales[:, t, :],
                rhs=hid_codes[:].bitcast(E5M2),
                rhs_scale=hid_scales[:],
                start=True,
                stop=True,
            )
            nc.scalar.activation(out=diff[:, t, :], in_=acc_p[:], func=ACT.Identity, bias=neg_hi[:, t : t + 1], scale=1.0)
            nc.vector.scalar_tensor_tensor(
                out=y[:, t, :], in0=diff[:, t, :], scalar=0.0, in1=rw_rows[:], op0=ALU.min, op1=ALU.mult
            )
        nc.sync.dma_start(out=out_0.rearrange("(p t) g -> p t g", t=PACK), in_=y[:])

        y_bf = sb.tile([P, G, PACK], BF16, name="y_bf", align_bytes=64)
        for v in range(2):
            nc.vector.tensor_copy(out=y_bf[:, :, 2 * v : 2 * v + 2], in_=y[:, 2 * v : 2 * v + 2, :].rearrange("p t g -> p g t"))
        y_codes = sb.tile([P, G], I32, name="y_codes", align_bytes=64)
        y_scales = sb.tile([P, G], U8, name="y_scales", align_bytes=64)
        nc.vector.quantize_mx(out=y_codes[:].bitcast(E4M3), scales=y_scales[:], in_=y_bf[:].rearrange("p g t -> p (g t)"))
        nc.sync.dma_start(out=out_1[0].rearrange("p g t -> p (g t)").bitcast(I32), in_=y_codes[:])
        for q in range(4):
            queue = nc.scalar if q < 2 else nc.sync
            queue.dma_start(out=out_2[0, 4 * q : 4 * q + 4, :].bitcast(I32), in_=y_scales[32 * q : 32 * q + 4, :].bitcast(I32))
